import numpy as np
import ml_dtypes


def mxq(x, axis, fmt="e4m3"):
    dtype, down = {"e4m3": (ml_dtypes.float8_e4m3fn, 7), "e5m2": (ml_dtypes.float8_e5m2, 14)}[fmt]
    v = np.moveaxis(np.asarray(x, np.float32).astype(ml_dtypes.bfloat16).astype(np.float64), axis, -1)
    blocks = v.reshape(v.shape[:-1] + (-1, 32))
    amax = np.abs(blocks).max(-1, keepdims=True)
    byte = np.maximum(np.where(amax > 0, np.frexp(amax)[1] - 1 + 127, 0) - down, 1)
    scale = np.exp2(byte - 127.0)
    codes = (blocks / scale).astype(np.float32).astype(dtype).astype(np.float64)
    return np.moveaxis((codes * scale).reshape(v.shape), -1, axis)


WIDE = False


def mx_kscale(k):
    if not WIDE:
        return np.ones(k)
    levels = np.array([10, -10, 5, -5, 0])
    if k % 512:
        return np.exp2(np.random.permutation(np.resize(levels, k // 32))).repeat(32)
    a = np.empty((k // 512, 16))
    for p in range(k // 512):
        a[p, :8] = np.random.permutation(np.resize(levels, 8))
        for g in range(8):
            far = levels[np.abs(levels - a[p, g]) >= 10]
            a[p, g + 8] = far[np.random.randint(len(far))]
    return np.exp2(a.ravel()).repeat(32)


def f64(x):
    return np.asarray(x).astype(np.float64)


def striped(idx):
    return np.tile(idx.reshape(-1, 16).T, (8, 1)).astype(np.uint16)


def unstriped(offs):
    return offs[:16].T.reshape(-1).astype(np.int64)


def pack_weight(w):
    k, n = w.shape
    w = f64(np.asarray(w, np.float32).astype(ml_dtypes.bfloat16)).reshape(k // 32, 32, n)
    amax = np.abs(w).max(1)
    byte = np.clip(np.where(amax > 0, np.frexp(amax)[1] - 1 + 127 - 7, 1), 1, 254)
    scaled = (w * np.exp2(127.0 - byte)[:, None, :]).reshape(k, n).astype(np.float32)
    words = np.ascontiguousarray(scaled.reshape(k // 512, 128, 4, n).transpose(0, 1, 3, 2)).astype(ml_dtypes.float8_e4m3fn).view(np.uint8)
    return words, np.ascontiguousarray(byte.astype(np.uint8).reshape(k // 512, 16, n))


def unpack_weight(words, scales):
    g, p, n, _ = words.shape
    vals = np.ascontiguousarray(words).view(ml_dtypes.float8_e4m3fn).astype(np.float64) * np.repeat(np.exp2(scales.astype(np.float64) - 127.0), 8, axis=1)[..., None]
    return vals.transpose(0, 1, 3, 2).reshape(g * 512, n)


def planes(y):
    n, m = y.shape
    v = y.astype(np.float32).astype(ml_dtypes.bfloat16).astype(np.float64).reshape(n // 32, 32, m)
    top = np.abs(v).max(1)
    byte = np.clip(np.where(top > 0, np.frexp(top)[1] - 1 + 127 - 7, 1), 1, 254)
    codes = (v * np.exp2(127.0 - byte)[:, None, :]).reshape(n, m).astype(np.float32).astype(ml_dtypes.float8_e4m3fn).view(np.uint8)
    words = codes.reshape(n // 512, 128, 4, m).transpose(0, 1, 3, 2)
    return np.ascontiguousarray(words), np.ascontiguousarray(byte.astype(np.uint8).reshape(n // 512, 16, m))


K, T, S, V, H, N = 512, 2048, 512, 256, 512, 512


def setup_inputs():
    n = np.random.standard_normal
    s = mx_kscale(K)[:, None]
    u = mx_kscale(H)
    near = np.random.permutation(S)
    packed_xT = pack_weight(n((K, T)) * s)
    packed_w1 = pack_weight(n((K, N)) / np.sqrt(K) / s)
    packed_w2 = pack_weight(n((K, N)) / np.sqrt(K) / s)
    packed_w4 = pack_weight(n((H, N)) / np.sqrt(H) / u[:, None])
    return {
        "x_words": packed_xT[0],
        "x_scales": packed_xT[1],
        "w1_words": packed_w1[0],
        "w1_scales": packed_w1[1],
        "w2_words": packed_w2[0],
        "w2_scales": packed_w2[1],
        "w3": (n((K, H)) / np.sqrt(K) / s * u).astype(np.float32),
        "w4_words": packed_w4[0],
        "w4_scales": packed_w4[1],
        "offs": striped(np.random.permutation(T)[:S]),
        "cen": striped(np.random.permutation(S)[:V]),
        "pos1": striped(near[:V]),
        "pos2": striped(near[V:]),
        "pos3": striped(np.random.permutation(S)[:V]),
    }


def reference(x_words, x_scales, w1_words, w1_scales, w2_words, w2_scales, w3, w4_words, w4_scales, offs, cen, pos1, pos2, pos3):
    xq = unpack_weight(x_words, x_scales)[:, unstriped(offs)]
    h = mxq(f64(w3), 0, "e4m3").T @ xq
    e = unpack_weight(w2_words, w2_scales).T @ xq
    y = unpack_weight(w1_words, w1_scales).T @ xq
    yc = y[:, unstriped(cen)]
    a0 = np.exp(np.tanh(e[:, unstriped(pos1)] * yc))
    a1 = np.exp(np.tanh(e[:, unstriped(pos2)] * yc))
    a2 = np.exp(np.tanh(e[:, unstriped(pos3)] * yc))
    num = h[:, unstriped(pos1)] * a0 + h[:, unstriped(pos2)] * a1 + h[:, unstriped(pos3)] * a2
    den = a0 + a1 + a2
    z = num / den
    out_0 = unpack_weight(w4_words, w4_scales).T @ mxq(z, 0, "e4m3")
    return (out_0,) + planes(out_0)

@@ -1,0 +1,233 @@
+from contextlib import ExitStack
+
+import concourse.mybir as mybir
+from concourse.masks import make_identity
+
+K, T, S, V, N = 512, 2048, 512, 256, 512
+FLOPS = 3 * 2 * K * N * S + 2 * N * N * V
+
+F32 = mybir.dt.float32
+BF16 = mybir.dt.bfloat16
+I32 = mybir.dt.int32
+U32 = mybir.dt.uint32
+U16 = mybir.dt.uint16
+U8 = mybir.dt.uint8
+FP8X4 = mybir.dt.float8_e4m3fn_x4
+ACT = mybir.ActivationFunctionType
+MULT = mybir.AluOpType.mult
+
+P = 128
+PACK = 4
+TILES = N // P
+HALVES = V // P
+D = 3
+
+
+def tile_picked_zpt_mul_po_kernel(
+    tc, x_words, x_scales, w1_words, w1_scales, w2_words, w2_scales, w3, w4_words, w4_scales,
+    offs, cen, pos1, pos2, pos3, out_0, out_1, out_2,
+):
+    nc = tc.nc
+
+    def words_of(dram):
+        return dram[0].rearrange("p n t -> p (n t)").bitcast(I32)
+
+    def load_scales(queue, plane, dram):
+        for q in range(4):
+            queue.dma_start(out=plane[32 * q : 32 * q + 4, :].bitcast(I32), in_=dram[0, 4 * q : 4 * q + 4, :].bitcast(I32))
+
+    def mx(out, w_words, w_scale, r_words, r_scale):
+        nc.tensor.matmul_mx(out=out, lhsT=w_words.bitcast(FP8X4), lhsT_scale=w_scale,
+                            rhs=r_words.bitcast(FP8X4), rhs_scale=r_scale, start=True, stop=True)
+
+    with ExitStack() as ctx:
+        keep = ctx.enter_context(tc.tile_pool(name="keep", bufs=1))
+        psum = ctx.enter_context(tc.psum_pool(name="psum", bufs=1))
+
+        def sb(name, shape, dtype, tag=None):
+            return keep.tile(shape, dtype, name=name, tag=tag or name, align_bytes=64)
+
+        def bank(name):
+            return psum.tile([P, 512], F32, name=name, tag="ring", bufs=4)
+
+        offs_t = sb("offs_t", [P, S // 16], U16)
+        nc.sync.dma_start(offs_t[:], offs)
+        xw = sb("xw", [P, T], U32)
+        nc.sync.dma_start(out=xw[:].bitcast(I32), in_=words_of(x_words))
+        xs = sb("xs", [P, T], U8)
+        nc.vector.memset(xs[:].bitcast(I32), 0)
+        load_scales(nc.scalar, xs, x_scales)
+
+        w1s = sb("w1s", [P, N], U8)
+        w2s = sb("w2s", [P, N], U8)
+        w4s = sb("w4s", [P, N], U8)
+        nc.gpsimd.memset(w2s[:].bitcast(I32), 0)
+        load_scales(nc.gpsimd, w2s, w2_scales)
+        nc.vector.memset(w1s[:].bitcast(I32), 0)
+        nc.vector.memset(w4s[:].bitcast(I32), 0)
+
+        w3_rows = w3.rearrange("(p j) n -> p j n", j=PACK)
+        w3raw = []
+        for c in range(2):
+            raw = sb(f"w3raw{c}", [P, PACK, 256], F32)
+            nc.sync.dma_start(out=raw[:], in_=w3_rows[:, :, 256 * c : 256 * (c + 1)])
+            w3raw.append(raw)
+        load_scales(nc.sync, w1s, w1_scales)
+        w1w = sb("w1w", [P, N], U32)
+        nc.sync.dma_start(out=w1w[:].bitcast(I32), in_=words_of(w1_words))
+        w2w = sb("w2w", [P, N], U32)
+        nc.sync.dma_start(out=w2w[:].bitcast(I32), in_=words_of(w2_words))
+        cen_t = sb("cen_t", [P, V // 16], U16)
+        nc.sync.dma_start(cen_t[:], cen)
+        pos_t = []
+        for d, pos in enumerate((pos1, pos2, pos3)):
+            lst = sb(f"pos_t{d}", [P, V // 16], U16)
+            nc.sync.dma_start(lst[:], pos)
+            pos_t.append(lst)
+        w4w = sb("w4w", [P, N], U32)
+        nc.sync.dma_start(out=w4w[:].bitcast(I32), in_=words_of(w4_words))
+        load_scales(nc.sync, w4s, w4_scales)
+
+        ident = sb("ident", [P, P], F32)
+        make_identity(nc, ident[:])
+
+        xqs = sb("xqs", [P, S], U8)
+        nc.vector.tensor_copy(xqs[:], xs[:].indirect(offs_t[:]))
+        xq = sb("xq", [P, S], U32)
+        nc.vector.tensor_copy(xq[:], xw[:].indirect(offs_t[:]))
+
+        w3w, w3s = [], []
+        for c in range(2):
+            grouped = sb(f"w3g{c}", [P, 256, PACK], BF16)
+            nc.scalar.activation(out=grouped[:].rearrange("p (c i) j -> p c j i", i=4),
+                                 in_=w3raw[c][:].rearrange("p j (c i) -> p c j i", i=4), func=ACT.Copy)
+            codes = sb(f"w3w{c}", [P, 256], U32)
+            plane = sb(f"w3s{c}", [P, 256], U8)
+            nc.vector.quantize_mx(out=codes[:].bitcast(FP8X4), scales=plane[:], in_=grouped[:].rearrange("p n j -> p (n j)"))
+            w3w.append(codes)
+            w3s.append(plane)
+
+        den = [psum.tile([P, N], F32, name=f"den{hv}") for hv in range(HALVES)]
+        num = [psum.tile([P, N], F32, name=f"num{hv}") for hv in range(HALVES)]
+        h = [None] * TILES
+        a = [None] * TILES
+
+        def add_turned(acc, terms, t):
+            for d in range(D):
+                for hv in range(HALVES):
+                    nc.tensor.matmul(out=acc[hv][:, P * t : P * (t + 1)],
+                                     lhsT=terms[:, d, P * hv : P * (hv + 1)], rhs=ident[:],
+                                     is_transpose=True, start=(d == 0), stop=(d == D - 1))
+
+        def value_rows(t, copy):
+            cols = slice(P * (t % 2), P * (t % 2 + 1))
+            acc = bank(f"h_ps{t}")
+            mx(acc[:], w3w[t // 2][:, cols], w3s[t // 2][:, cols], xq[:], xqs[:])
+            h_t = sb(f"h{t}", [P, S], F32)
+            copy(h_t[:], acc[:])
+            h[t] = h_t
+
+        def scores(t):
+            cols = slice(P * t, P * (t + 1))
+            y_ps = bank(f"y_ps{t}")
+            mx(y_ps[:], w1w[:, cols], w1s[:, cols], xq[:], xqs[:])
+            e_ps = bank(f"e_ps{t}")
+            mx(e_ps[:], w2w[:, cols], w2s[:, cols], xq[:], xqs[:])
+            y_t = sb(f"y{t}", [P, S], F32)
+            nc.scalar.copy(y_t[:], y_ps[:])
+            e_t = sb(f"e{t}", [P, S], F32)
+            nc.vector.tensor_copy(e_t[:], e_ps[:])
+            yc = sb(f"yc{t}", [P, V], F32)
+            nc.scalar.activation(out=yc[:], in_=y_t[:].indirect(cen_t[:]), func=ACT.Copy)
+            s_t = sb(f"s{t}", [P, D, V], F32)
+            for d in range(D):
+                nc.vector.tensor_tensor(s_t[:, d, :], e_t[:].indirect(pos_t[d][:]), yc[:], MULT)
+            return s_t
+
+        def weights(t, s_t):
+            th = sb(f"th{t}", [P, D * V], F32)
+            nc.scalar.activation(out=th[:], in_=s_t[:].rearrange("p d v -> p (d v)"), func=ACT.Tanh)
+            a_t = sb(f"a{t}", [P, D, V], F32)
+            nc.scalar.activation(out=a_t[:].rearrange("p d v -> p (d v)"), in_=th[:], func=ACT.Exp)
+            add_turned(den, a_t, t)
+            a[t] = a_t
+
+        value_rows(0, nc.vector.tensor_copy)
+        value_rows(1, nc.vector.tensor_copy)
+        s0 = scores(0)
+        s1 = scores(1)
+        value_rows(2, nc.scalar.copy)
+        weights(0, s0)
+        s2 = scores(2)
+        weights(1, s1)
+        s3 = scores(3)
+        weights(2, s2)
+        weights(3, s3)
+        value_rows(3, nc.scalar.copy)
+
+        logs, inv = [], []
+        for hv in range(HALVES):
+            lg = sb(f"log{hv}", [P, N], F32)
+            nc.scalar.activation(out=lg[:], in_=den[hv][:], func=ACT.Ln)
+            logs.append(lg)
+        for hv in range(HALVES):
+            iv = sb(f"inv{hv}", [P, N], F32)
+            nc.scalar.activation(out=iv[:], in_=logs[hv][:], func=ACT.Exp, scale=-1.0)
+            inv.append(iv)
+
+        prod = sb("prod", [P, TILES, D, V], F32, tag=f"e{TILES - 1}")
+        for t in range(TILES):
+            for d in range(D):
+                nc.vector.tensor_tensor(prod[:, t, d, :], h[t][:].indirect(pos_t[d][:]), a[t][:, d, :], MULT)
+            add_turned(num, prod[:, t], t)
+
+        w4wd = sb("w4wd", [P, TILES, P], U32, tag="log0")
+        nc.scalar.copy(w4wd[:].rearrange("p t (c i) -> p c t i", i=4),
+                       w4w[:].rearrange("p (c i t) -> p c t i", i=4, t=4))
+
+        z = []
+        for hv in range(HALVES):
+            z_hv = sb(f"z{hv}", [P, N], BF16)
+            nc.vector.tensor_tensor(z_hv[:], num[hv][:], inv[hv][:], MULT)
+            z.append(z_hv)
+        w4sd = sb("w4sd", [P, TILES, P], U8, tag="inv1")
+        nc.vector.tensor_copy(w4sd[:].rearrange("p t (c i) -> p c t i", i=16),
+                              w4s[:].rearrange("p (c i t) -> p c t i", i=16, t=4))
+
+        oq = sb("oq", [P, V], U32)
+        osc = sb("osc", [P, V], U8)
+        out_rows = out_0.rearrange("(p t) v -> p t v", t=TILES)
+        zq = []
+        for hv in range(HALVES):
+            zt = bank(f"zt{hv}")
+            words = z[hv][:].bitcast(F32)
+            for u in range(2):
+                nc.tensor.transpose(zt[:, P * u : P * (u + 1)], words[:, u : 2 * P : 2], ident[:])
+            zg = sb(f"zg{hv}", [P, P, 2], F32)
+            turned = zt[:, 0 : 2 * P].rearrange("p (u v) -> p v u", u=2)
+            nc.scalar.copy(zg[:], turned)
+            zq.append(zg)
+        o_ps = []
+        for hv in range(HALVES):
+            zw = sb(f"zw{hv}", [P, P], U32)
+            zs = sb(f"zs{hv}", [P, P], U8)
+            nc.vector.quantize_mx(out=zw[:].bitcast(FP8X4), scales=zs[:],
+                                  in_=zq[hv][:].rearrange("p v u -> p (v u)").bitcast(BF16))
+            acc = bank(f"o_ps{hv}")
+            for t in range(TILES):
+                mx(acc[:, P * t : P * (t + 1)], w4wd[:, t, :], w4sd[:, t, :], zw[:], zs[:])
+            o_ps.append(acc)
+        for hv in range(HALVES):
+            cols = slice(P * hv, P * (hv + 1))
+            o32 = sb(f"o32_{hv}", [P, TILES, P], F32)
+            nc.scalar.copy(o32[:].rearrange("p t v -> p (t v)"), o_ps[hv][:])
+            nc.sync.dma_start(out=out_rows[:, :, cols], in_=o32[:])
+            ob = sb(f"ob{hv}", [P, P, PACK], BF16)
+            nc.vector.tensor_copy(ob[:].rearrange("p (c i) t -> p c t i", i=4),
+                                  o32[:].rearrange("p t (c i) -> p c t i", i=4))
+            nc.vector.quantize_mx(out=oq[:, cols].bitcast(FP8X4), scales=osc[:, cols],
+                                  in_=ob[:].rearrange("p v t -> p (v t)"))
+        nc.sync.dma_start(out=words_of(out_1), in_=oq[:].bitcast(I32))
+        for q in range(4):
+            queue = nc.scalar if q % 2 else nc.sync
+            queue.dma_start(out=out_2[0, 4 * q : 4 * q + 4, :].bitcast(I32), in_=osc[32 * q : 32 * q + 4, :].bitcast(I32))

@@ -56,7 +56,7 @@ def tile_picked_zpt_mul_po_kernel(
         nc.sync.dma_start(out=xw[:].bitcast(I32), in_=words_of(x_words))
         xs = sb("xs", [P, T], U8)
         nc.vector.memset(xs[:].bitcast(I32), 0)
-        load_scales(nc.scalar, xs, x_scales)
+        load_scales(nc.sync, xs, x_scales)
 
         w1s = sb("w1s", [P, N], U8)
         w2s = sb("w2s", [P, N], U8)
@@ -116,7 +116,7 @@ def tile_picked_zpt_mul_po_kernel(
             for d in range(D):
                 for hv in range(HALVES):
                     nc.tensor.matmul(out=acc[hv][:, P * t : P * (t + 1)],
-                                     lhsT=terms[:, d, P * hv : P * (hv + 1)], rhs=ident[:],
+                                     lhsT=terms[d][:, P * hv : P * (hv + 1)], rhs=ident[:],
                                      is_transpose=True, start=(d == 0), stop=(d == D - 1))
 
         def value_rows(t, copy):
@@ -127,7 +127,7 @@ def tile_picked_zpt_mul_po_kernel(
             copy(h_t[:], acc[:])
             h[t] = h_t
 
-        def scores(t):
+        def scores(t, copy_keys):
             cols = slice(P * t, P * (t + 1))
             y_ps = bank(f"y_ps{t}")
             mx(y_ps[:], w1w[:, cols], w1s[:, cols], xq[:], xqs[:])
@@ -136,7 +136,7 @@ def tile_picked_zpt_mul_po_kernel(
             y_t = sb(f"y{t}", [P, S], F32)
             nc.scalar.copy(y_t[:], y_ps[:])
             e_t = sb(f"e{t}", [P, S], F32)
-            nc.vector.tensor_copy(e_t[:], e_ps[:])
+            copy_keys(e_t[:], e_ps[:])
             yc = sb(f"yc{t}", [P, V], F32)
             nc.scalar.activation(out=yc[:], in_=y_t[:].indirect(cen_t[:]), func=ACT.Copy)
             s_t = sb(f"s{t}", [P, D, V], F32)
@@ -149,39 +149,43 @@ def tile_picked_zpt_mul_po_kernel(
             nc.scalar.activation(out=th[:], in_=s_t[:].rearrange("p d v -> p (d v)"), func=ACT.Tanh)
             a_t = sb(f"a{t}", [P, D, V], F32)
             nc.scalar.activation(out=a_t[:].rearrange("p d v -> p (d v)"), in_=th[:], func=ACT.Exp)
-            add_turned(den, a_t, t)
+            add_turned(den, [a_t[:, d, :] for d in range(D)], t)
             a[t] = a_t
 
+        s0 = scores(0, nc.vector.tensor_copy)
         value_rows(0, nc.vector.tensor_copy)
-        value_rows(1, nc.vector.tensor_copy)
-        s0 = scores(0)
-        s1 = scores(1)
-        value_rows(2, nc.scalar.copy)
+        s1 = scores(1, nc.scalar.copy)
+        s2 = scores(2, nc.vector.tensor_copy)
         weights(0, s0)
-        s2 = scores(2)
+        s3 = scores(3, nc.vector.tensor_copy)
         weights(1, s1)
-        s3 = scores(3)
+        value_rows(1, nc.scalar.copy)
         weights(2, s2)
         weights(3, s3)
+        value_rows(2, nc.scalar.copy)
         value_rows(3, nc.scalar.copy)
 
-        logs, inv = [], []
+        inv = []
         for hv in range(HALVES):
-            lg = sb(f"log{hv}", [P, N], F32)
-            nc.scalar.activation(out=lg[:], in_=den[hv][:], func=ACT.Ln)
-            logs.append(lg)
-        for hv in range(HALVES):
+            root = sb(f"log{hv}", [P, N], F32)
+            nc.scalar.activation(out=root[:], in_=den[hv][:], func=ACT.Abs_reciprocal_sqrt)
             iv = sb(f"inv{hv}", [P, N], F32)
-            nc.scalar.activation(out=iv[:], in_=logs[hv][:], func=ACT.Exp, scale=-1.0)
+            nc.scalar.activation(out=iv[:], in_=root[:], func=ACT.Square)
             inv.append(iv)
 
-        prod = sb("prod", [P, TILES, D, V], F32, tag=f"e{TILES - 1}")
+        early = 5
+        first = sb("prod_first", [P, early, V], F32, tag=f"e{TILES - 1}")
+        rest = sb("prod_rest", [P, TILES * D - early, V], F32, tag=f"th{TILES - 1}")
         for t in range(TILES):
+            terms = []
             for d in range(D):
-                nc.vector.tensor_tensor(prod[:, t, d, :], h[t][:].indirect(pos_t[d][:]), a[t][:, d, :], MULT)
-            add_turned(num, prod[:, t], t)
+                n = D * t + d
+                prod = first[:, n, :] if n < early else rest[:, n - early, :]
+                nc.vector.tensor_tensor(prod, h[t][:].indirect(pos_t[d][:]), a[t][:, d, :], MULT)
+                terms.append(prod)
+            add_turned(num, terms, t)
 
-        w4wd = sb("w4wd", [P, TILES, P], U32, tag="log0")
+        w4wd = sb("w4wd", [P, TILES, P], U32, tag="log1")
         nc.scalar.copy(w4wd[:].rearrange("p t (c i) -> p c t i", i=4),
                        w4w[:].rearrange("p (c i t) -> p c t i", i=4, t=4))
 
@@ -217,16 +221,18 @@ def tile_picked_zpt_mul_po_kernel(
             for t in range(TILES):
                 mx(acc[:, P * t : P * (t + 1)], w4wd[:, t, :], w4sd[:, t, :], zw[:], zs[:])
             o_ps.append(acc)
+        rounded = []
+        for hv, copy in enumerate((nc.scalar.copy, nc.vector.tensor_copy)):
+            ob = sb(f"ob{hv}", [P, P, PACK], BF16)
+            copy(ob[:], o_ps[hv][:].rearrange("p (t v) -> p v t", t=TILES))
+            rounded.append(ob)
         for hv in range(HALVES):
             cols = slice(P * hv, P * (hv + 1))
             o32 = sb(f"o32_{hv}", [P, TILES, P], F32)
             nc.scalar.copy(o32[:].rearrange("p t v -> p (t v)"), o_ps[hv][:])
             nc.sync.dma_start(out=out_rows[:, :, cols], in_=o32[:])
-            ob = sb(f"ob{hv}", [P, P, PACK], BF16)
-            nc.vector.tensor_copy(ob[:].rearrange("p (c i) t -> p c t i", i=4),
-                                  o32[:].rearrange("p t (c i) -> p c t i", i=4))
             nc.vector.quantize_mx(out=oq[:, cols].bitcast(FP8X4), scales=osc[:, cols],
-                                  in_=ob[:].rearrange("p v t -> p (v t)"))
+                                  in_=rounded[hv][:].rearrange("p v t -> p (v t)"))
         nc.sync.dma_start(out=words_of(out_1), in_=oq[:].bitcast(I32))
         for q in range(4):
             queue = nc.scalar if q % 2 else nc.sync

@@ -33,8 +33,8 @@ def tile_picked_zpt_mul_po_kernel(
         return dram[0].rearrange("p n t -> p (n t)").bitcast(I32)
 
     def load_scales(queue, plane, dram):
-        for q in range(4):
-            queue.dma_start(out=plane[32 * q : 32 * q + 4, :].bitcast(I32), in_=dram[0, 4 * q : 4 * q + 4, :].bitcast(I32))
+        for r in range(4):
+            queue.dma_start(out=plane[r:P:32, :].bitcast(I32), in_=dram[0, r:16:4, :].bitcast(I32))
 
     def mx(out, w_words, w_scale, r_words, r_scale):
         nc.tensor.matmul_mx(out=out, lhsT=w_words.bitcast(FP8X4), lhsT_scale=w_scale,
@@ -155,7 +155,7 @@ def tile_picked_zpt_mul_po_kernel(
         s0 = scores(0, nc.vector.tensor_copy)
         value_rows(0, nc.vector.tensor_copy)
         s1 = scores(1, nc.scalar.copy)
-        s2 = scores(2, nc.vector.tensor_copy)
+        s2 = scores(2, nc.scalar.copy)
         weights(0, s0)
         s3 = scores(3, nc.vector.tensor_copy)
         weights(1, s1)
@@ -173,7 +173,7 @@ def tile_picked_zpt_mul_po_kernel(
             nc.scalar.activation(out=iv[:], in_=root[:], func=ACT.Square)
             inv.append(iv)
 
-        early = 5
+        early = 6
         first = sb("prod_first", [P, early, V], F32, tag=f"e{TILES - 1}")
         rest = sb("prod_rest", [P, TILES * D - early, V], F32, tag=f"th{TILES - 1}")
         for t in range(TILES):
@@ -189,14 +189,17 @@ def tile_picked_zpt_mul_po_kernel(
         nc.scalar.copy(w4wd[:].rearrange("p t (c i) -> p c t i", i=4),
                        w4w[:].rearrange("p (c i t) -> p c t i", i=4, t=4))
 
+        w4sd = sb("w4sd", [P, TILES, P], U8, tag="h3")
+        nc.vector.tensor_copy(w4sd[:].rearrange("p t (c i) -> p c t i", i=16),
+                              w4s[:].rearrange("p (c i t) -> p c t i", i=16, t=4))
+
         z = []
         for hv in range(HALVES):
             z_hv = sb(f"z{hv}", [P, N], BF16)
-            nc.vector.tensor_tensor(z_hv[:], num[hv][:], inv[hv][:], MULT)
+            nc.vector.tensor_tensor(z_hv[:].rearrange("p (u q e) -> p u q e", u=2, e=2),
+                                    num[hv][:].rearrange("p (q u e) -> p u q e", u=2, e=2),
+                                    inv[hv][:].rearrange("p (q u e) -> p u q e", u=2, e=2), MULT)
             z.append(z_hv)
-        w4sd = sb("w4sd", [P, TILES, P], U8, tag="inv1")
-        nc.vector.tensor_copy(w4sd[:].rearrange("p t (c i) -> p c t i", i=16),
-                              w4s[:].rearrange("p (c i t) -> p c t i", i=16, t=4))
 
         oq = sb("oq", [P, V], U32)
         osc = sb("osc", [P, V], U8)
@@ -206,7 +209,7 @@ def tile_picked_zpt_mul_po_kernel(
             zt = bank(f"zt{hv}")
             words = z[hv][:].bitcast(F32)
             for u in range(2):
-                nc.tensor.transpose(zt[:, P * u : P * (u + 1)], words[:, u : 2 * P : 2], ident[:])
+                nc.tensor.transpose(zt[:, P * u : P * (u + 1)], words[:, P * u : P * (u + 1)], ident[:])
             zg = sb(f"zg{hv}", [P, P, 2], F32)
             turned = zt[:, 0 : 2 * P].rearrange("p (u v) -> p v u", u=2)
             nc.scalar.copy(zg[:], turned)

@@ -232,8 +232,9 @@ def tile_picked_zpt_mul_po_kernel(
         for hv in range(HALVES):
             cols = slice(P * hv, P * (hv + 1))
             o32 = sb(f"o32_{hv}", [P, TILES, P], F32)
-            nc.scalar.copy(o32[:].rearrange("p t v -> p (t v)"), o_ps[hv][:])
-            nc.sync.dma_start(out=out_rows[:, :, cols], in_=o32[:])
+            for rows in ((slice(0, 4),), (slice(0, 2), slice(2, 4)))[hv]:
+                nc.scalar.copy(o32[:, rows, :], o_ps[hv][:].rearrange("p (t v) -> p t v", t=TILES)[:, rows, :])
+                nc.sync.dma_start(out=out_rows[:, rows, cols], in_=o32[:, rows, :])
             nc.vector.quantize_mx(out=oq[:, cols].bitcast(FP8X4), scales=osc[:, cols],
                                   in_=rounded[hv][:].rearrange("p v t -> p (v t)"))
         nc.sync.dma_start(out=words_of(out_1), in_=oq[:].bitcast(I32))

from contextlib import ExitStack

import concourse.mybir as mybir
from concourse.masks import make_identity

K, T, S, V, N = 512, 2048, 512, 256, 512
FLOPS = 3 * 2 * K * N * S + 2 * N * N * V

F32 = mybir.dt.float32
BF16 = mybir.dt.bfloat16
I32 = mybir.dt.int32
U32 = mybir.dt.uint32
U16 = mybir.dt.uint16
U8 = mybir.dt.uint8
FP8X4 = mybir.dt.float8_e4m3fn_x4
ACT = mybir.ActivationFunctionType
MULT = mybir.AluOpType.mult

P = 128
PACK = 4
TILES = N // P
HALVES = V // P
D = 3


def tile_picked_zpt_mul_po_kernel(
    tc, x_words, x_scales, w1_words, w1_scales, w2_words, w2_scales, w3, w4_words, w4_scales,
    offs, cen, pos1, pos2, pos3, out_0, out_1, out_2,
):
    nc = tc.nc

    def words_of(dram):
        return dram[0].rearrange("p n t -> p (n t)").bitcast(I32)

    def load_scales(queue, plane, dram):
        for r in range(4):
            queue.dma_start(out=plane[r:P:32, :].bitcast(I32), in_=dram[0, r:16:4, :].bitcast(I32))

    def mx(out, w_words, w_scale, r_words, r_scale):
        nc.tensor.matmul_mx(out=out, lhsT=w_words.bitcast(FP8X4), lhsT_scale=w_scale,
                            rhs=r_words.bitcast(FP8X4), rhs_scale=r_scale, start=True, stop=True)

    with ExitStack() as ctx:
        keep = ctx.enter_context(tc.tile_pool(name="keep", bufs=1))
        psum = ctx.enter_context(tc.psum_pool(name="psum", bufs=1))

        def sb(name, shape, dtype, tag=None):
            return keep.tile(shape, dtype, name=name, tag=tag or name, align_bytes=64)

        def bank(name):
            return psum.tile([P, 512], F32, name=name, tag="ring", bufs=4)

        offs_t = sb("offs_t", [P, S // 16], U16)
        nc.sync.dma_start(offs_t[:], offs)
        xw = sb("xw", [P, T], U32)
        nc.sync.dma_start(out=xw[:].bitcast(I32), in_=words_of(x_words))
        xs = sb("xs", [P, T], U8)
        nc.vector.memset(xs[:].bitcast(I32), 0)
        load_scales(nc.sync, xs, x_scales)

        w1s = sb("w1s", [P, N], U8)
        w2s = sb("w2s", [P, N], U8)
        w4s = sb("w4s", [P, N], U8)
        nc.gpsimd.memset(w2s[:].bitcast(I32), 0)
        load_scales(nc.gpsimd, w2s, w2_scales)
        nc.vector.memset(w1s[:].bitcast(I32), 0)
        nc.vector.memset(w4s[:].bitcast(I32), 0)

        w3_rows = w3.rearrange("(p j) n -> p j n", j=PACK)
        w3raw = []
        for c in range(2):
            raw = sb(f"w3raw{c}", [P, PACK, 256], F32)
            nc.sync.dma_start(out=raw[:], in_=w3_rows[:, :, 256 * c : 256 * (c + 1)])
            w3raw.append(raw)
        load_scales(nc.sync, w1s, w1_scales)
        w1w = sb("w1w", [P, N], U32)
        nc.sync.dma_start(out=w1w[:].bitcast(I32), in_=words_of(w1_words))
        w2w = sb("w2w", [P, N], U32)
        nc.sync.dma_start(out=w2w[:].bitcast(I32), in_=words_of(w2_words))
        cen_t = sb("cen_t", [P, V // 16], U16)
        nc.sync.dma_start(cen_t[:], cen)
        pos_t = []
        for d, pos in enumerate((pos1, pos2, pos3)):
            lst = sb(f"pos_t{d}", [P, V // 16], U16)
            nc.sync.dma_start(lst[:], pos)
            pos_t.append(lst)
        w4w = sb("w4w", [P, N], U32)
        nc.sync.dma_start(out=w4w[:].bitcast(I32), in_=words_of(w4_words))
        load_scales(nc.sync, w4s, w4_scales)

        ident = sb("ident", [P, P], F32)
        make_identity(nc, ident[:])

        xqs = sb("xqs", [P, S], U8)
        nc.vector.tensor_copy(xqs[:], xs[:].indirect(offs_t[:]))
        xq = sb("xq", [P, S], U32)
        nc.vector.tensor_copy(xq[:], xw[:].indirect(offs_t[:]))

        w3w, w3s = [], []
        for c in range(2):
            grouped = sb(f"w3g{c}", [P, 256, PACK], BF16)
            nc.scalar.activation(out=grouped[:].rearrange("p (c i) j -> p c j i", i=4),
                                 in_=w3raw[c][:].rearrange("p j (c i) -> p c j i", i=4), func=ACT.Copy)
            codes = sb(f"w3w{c}", [P, 256], U32)
            plane = sb(f"w3s{c}", [P, 256], U8)
            nc.vector.quantize_mx(out=codes[:].bitcast(FP8X4), scales=plane[:], in_=grouped[:].rearrange("p n j -> p (n j)"))
            w3w.append(codes)
            w3s.append(plane)

        den = [psum.tile([P, N], F32, name=f"den{hv}") for hv in range(HALVES)]
        num = [psum.tile([P, N], F32, name=f"num{hv}") for hv in range(HALVES)]
        h = [None] * TILES
        a = [None] * TILES

        def add_turned(acc, terms, t):
            for d in range(D):
                for hv in range(HALVES):
                    nc.tensor.matmul(out=acc[hv][:, P * t : P * (t + 1)],
                                     lhsT=terms[d][:, P * hv : P * (hv + 1)], rhs=ident[:],
                                     is_transpose=True, start=(d == 0), stop=(d == D - 1))

        def value_rows(t, copy):
            cols = slice(P * (t % 2), P * (t % 2 + 1))
            acc = bank(f"h_ps{t}")
            mx(acc[:], w3w[t // 2][:, cols], w3s[t // 2][:, cols], xq[:], xqs[:])
            h_t = sb(f"h{t}", [P, S], F32)
            copy(h_t[:], acc[:])
            h[t] = h_t

        def scores(t, copy_keys):
            cols = slice(P * t, P * (t + 1))
            y_ps = bank(f"y_ps{t}")
            mx(y_ps[:], w1w[:, cols], w1s[:, cols], xq[:], xqs[:])
            e_ps = bank(f"e_ps{t}")
            mx(e_ps[:], w2w[:, cols], w2s[:, cols], xq[:], xqs[:])
            y_t = sb(f"y{t}", [P, S], F32)
            nc.scalar.copy(y_t[:], y_ps[:])
            e_t = sb(f"e{t}", [P, S], F32)
            copy_keys(e_t[:], e_ps[:])
            yc = sb(f"yc{t}", [P, V], F32)
            nc.scalar.activation(out=yc[:], in_=y_t[:].indirect(cen_t[:]), func=ACT.Copy)
            s_t = sb(f"s{t}", [P, D, V], F32)
            for d in range(D):
                nc.vector.tensor_tensor(s_t[:, d, :], e_t[:].indirect(pos_t[d][:]), yc[:], MULT)
            return s_t

        def weights(t, s_t):
            th = sb(f"th{t}", [P, D * V], F32)
            nc.scalar.activation(out=th[:], in_=s_t[:].rearrange("p d v -> p (d v)"), func=ACT.Tanh)
            a_t = sb(f"a{t}", [P, D, V], F32)
            nc.scalar.activation(out=a_t[:].rearrange("p d v -> p (d v)"), in_=th[:], func=ACT.Exp)
            add_turned(den, [a_t[:, d, :] for d in range(D)], t)
            a[t] = a_t

        s0 = scores(0, nc.vector.tensor_copy)
        value_rows(0, nc.vector.tensor_copy)
        s1 = scores(1, nc.scalar.copy)
        s2 = scores(2, nc.scalar.copy)
        weights(0, s0)
        s3 = scores(3, nc.vector.tensor_copy)
        weights(1, s1)
        value_rows(1, nc.scalar.copy)
        weights(2, s2)
        weights(3, s3)
        value_rows(2, nc.scalar.copy)
        value_rows(3, nc.scalar.copy)

        inv = []
        for hv in range(HALVES):
            root = sb(f"log{hv}", [P, N], F32)
            nc.scalar.activation(out=root[:], in_=den[hv][:], func=ACT.Abs_reciprocal_sqrt)
            iv = sb(f"inv{hv}", [P, N], F32)
            nc.scalar.activation(out=iv[:], in_=root[:], func=ACT.Square)
            inv.append(iv)

        early = 6
        first = sb("prod_first", [P, early, V], F32, tag=f"e{TILES - 1}")
        rest = sb("prod_rest", [P, TILES * D - early, V], F32, tag=f"th{TILES - 1}")
        for t in range(TILES):
            terms = []
            for d in range(D):
                n = D * t + d
                prod = first[:, n, :] if n < early else rest[:, n - early, :]
                nc.vector.tensor_tensor(prod, h[t][:].indirect(pos_t[d][:]), a[t][:, d, :], MULT)
                terms.append(prod)
            add_turned(num, terms, t)

        w4wd = sb("w4wd", [P, TILES, P], U32, tag="log1")
        nc.scalar.copy(w4wd[:].rearrange("p t (c i) -> p c t i", i=4),
                       w4w[:].rearrange("p (c i t) -> p c t i", i=4, t=4))

        w4sd = sb("w4sd", [P, TILES, P], U8, tag="h3")
        nc.vector.tensor_copy(w4sd[:].rearrange("p t (c i) -> p c t i", i=16),
                              w4s[:].rearrange("p (c i t) -> p c t i", i=16, t=4))

        z = []
        for hv in range(HALVES):
            z_hv = sb(f"z{hv}", [P, N], BF16)
            nc.vector.tensor_tensor(z_hv[:].rearrange("p (u q e) -> p u q e", u=2, e=2),
                                    num[hv][:].rearrange("p (q u e) -> p u q e", u=2, e=2),
                                    inv[hv][:].rearrange("p (q u e) -> p u q e", u=2, e=2), MULT)
            z.append(z_hv)

        oq = sb("oq", [P, V], U32)
        osc = sb("osc", [P, V], U8)
        out_rows = out_0.rearrange("(p t) v -> p t v", t=TILES)
        zq = []
        for hv in range(HALVES):
            zt = bank(f"zt{hv}")
            words = z[hv][:].bitcast(F32)
            for u in range(2):
                nc.tensor.transpose(zt[:, P * u : P * (u + 1)], words[:, P * u : P * (u + 1)], ident[:])
            zg = sb(f"zg{hv}", [P, P, 2], F32)
            turned = zt[:, 0 : 2 * P].rearrange("p (u v) -> p v u", u=2)
            nc.scalar.copy(zg[:], turned)
            zq.append(zg)
        o_ps = []
        for hv in range(HALVES):
            zw = sb(f"zw{hv}", [P, P], U32)
            zs = sb(f"zs{hv}", [P, P], U8)
            nc.vector.quantize_mx(out=zw[:].bitcast(FP8X4), scales=zs[:],
                                  in_=zq[hv][:].rearrange("p v u -> p (v u)").bitcast(BF16))
            acc = bank(f"o_ps{hv}")
            for t in range(TILES):
                mx(acc[:, P * t : P * (t + 1)], w4wd[:, t, :], w4sd[:, t, :], zw[:], zs[:])
            o_ps.append(acc)
        rounded = []
        for hv, copy in enumerate((nc.scalar.copy, nc.vector.tensor_copy)):
            ob = sb(f"ob{hv}", [P, P, PACK], BF16)
            copy(ob[:], o_ps[hv][:].rearrange("p (t v) -> p v t", t=TILES))
            rounded.append(ob)
        for hv in range(HALVES):
            cols = slice(P * hv, P * (hv + 1))
            o32 = sb(f"o32_{hv}", [P, TILES, P], F32)
            for rows in ((slice(0, 4),), (slice(0, 2), slice(2, 4)))[hv]:
                nc.scalar.copy(o32[:, rows, :], o_ps[hv][:].rearrange("p (t v) -> p t v", t=TILES)[:, rows, :])
                nc.sync.dma_start(out=out_rows[:, rows, cols], in_=o32[:, rows, :])
            nc.vector.quantize_mx(out=oq[:, cols].bitcast(FP8X4), scales=osc[:, cols],
                                  in_=rounded[hv][:].rearrange("p v t -> p (v t)"))
        nc.sync.dma_start(out=words_of(out_1), in_=oq[:].bitcast(I32))
        for q in range(4):
            queue = nc.scalar if q % 2 else nc.sync
            queue.dma_start(out=out_2[0, 4 * q : 4 * q + 4, :].bitcast(I32), in_=osc[32 * q : 32 * q + 4, :].bitcast(I32))
